import numpy as np
import ml_dtypes


def mxq(x, axis, fmt="e4m3"):
    dtype, down = {"e4m3": (ml_dtypes.float8_e4m3fn, 7), "e5m2": (ml_dtypes.float8_e5m2, 14)}[fmt]
    v = np.moveaxis(np.asarray(x, np.float32).astype(ml_dtypes.bfloat16).astype(np.float64), axis, -1)
    blocks = v.reshape(v.shape[:-1] + (-1, 32))
    amax = np.abs(blocks).max(-1, keepdims=True)
    byte = np.maximum(np.where(amax > 0, np.frexp(amax)[1] - 1 + 127, 0) - down, 1)
    scale = np.exp2(byte - 127.0)
    codes = (blocks / scale).astype(np.float32).astype(dtype).astype(np.float64)
    return np.moveaxis((codes * scale).reshape(v.shape), -1, axis)


WIDE = False


def mx_kscale(k):
    if not WIDE:
        return np.ones(k)
    levels = np.array([10, -10, 5, -5, 0])
    if k % 512:
        return np.exp2(np.random.permutation(np.resize(levels, k // 32))).repeat(32)
    a = np.empty((k // 512, 16))
    for p in range(k // 512):
        a[p, :8] = np.random.permutation(np.resize(levels, 8))
        for g in range(8):
            far = levels[np.abs(levels - a[p, g]) >= 10]
            a[p, g + 8] = far[np.random.randint(len(far))]
    return np.exp2(a.ravel()).repeat(32)


def f64(x):
    return np.asarray(x).astype(np.float64)


def striped(idx):
    return np.tile(idx.reshape(-1, 16).T, (8, 1)).astype(np.uint16)


def unstriped(offs):
    return offs[:16].T.reshape(-1).astype(np.int64)


def pack_weight(w):
    k, n = w.shape
    w = f64(np.asarray(w, np.float32).astype(ml_dtypes.bfloat16)).reshape(k // 32, 32, n)
    amax = np.abs(w).max(1)
    byte = np.clip(np.where(amax > 0, np.frexp(amax)[1] - 1 + 127 - 7, 1), 1, 254)
    scaled = (w * np.exp2(127.0 - byte)[:, None, :]).reshape(k, n).astype(np.float32)
    words = np.ascontiguousarray(scaled.reshape(k // 512, 128, 4, n).transpose(0, 1, 3, 2)).astype(ml_dtypes.float8_e4m3fn).view(np.uint8)
    return words, np.ascontiguousarray(byte.astype(np.uint8).reshape(k // 512, 16, n))


def unpack_weight(words, scales):
    g, p, n, _ = words.shape
    vals = np.ascontiguousarray(words).view(ml_dtypes.float8_e4m3fn).astype(np.float64) * np.repeat(np.exp2(scales.astype(np.float64) - 127.0), 8, axis=1)[..., None]
    return vals.transpose(0, 1, 3, 2).reshape(g * 512, n)


K, T, S, N, H, U = 512, 1024, 512, 128, 512, 1024


def setup_inputs():
    n = np.random.standard_normal
    s = mx_kscale(K)[:, None]
    u = mx_kscale(H)
    packed_xT = pack_weight(n((K, T)) * s)
    return {
        "x_words": packed_xT[0],
        "x_scales": packed_xT[1],
        "w1": (n((K, H)) / np.sqrt(K) / s).astype(np.float32),
        "w2": (n((K, H)) / np.sqrt(K) / s).astype(np.float32),
        "por": (np.random.uniform(0.08, 0.35, (H, U))).astype(np.float32),
        "rho": (np.random.uniform(0.8, 1.2, (H, U))).astype(np.float32),
        "unit": (np.random.uniform(0.6, 1.4, (H, 1)) * u[:, None]).astype(np.float32),
        "w3": (n((H, N)) / np.sqrt(H) / u[:, None]).astype(np.float32),
        "offs": striped(np.random.permutation(T)[:S]),
        "rk": striped(np.random.permutation(np.concatenate([np.arange(S), np.random.randint(0, S, U - S)]))),
        "fl": striped(np.random.permutation(np.concatenate([np.arange(S), np.random.randint(0, S, U - S)]))),
    }


def reference(x_words, x_scales, w1, w2, por, rho, unit, w3, offs, rk, fl):
    xq = unpack_weight(x_words, x_scales)[:, unstriped(offs)]
    kd = mxq(f64(w1), 0, "e4m3").T @ xq
    kdry = np.log(np.exp(kd) + 1.0) + 0.4
    dr = kdry[:, unstriped(rk)]
    biot = -1.0 * (0.8 * (dr / (dr + 1.5))) + 1.0
    gd = mxq(f64(w2), 0, "e4m3").T @ xq
    kfl = 0.5 * (np.log(np.exp(gd) + 1.0)) + 0.1
    fr = kfl[:, unstriped(fl)]
    ksat = dr + ((biot) ** 2) / (f64(por) / fr + 0.3 * (biot - f64(por)))
    imp = np.sqrt(ksat * f64(rho))
    hid = f64(unit) * (imp - (0.8 * (np.repeat(imp.reshape(len(imp), -1, 4).mean(axis=2), 4, axis=1))))
    return mxq(f64(w3), 0, "e4m3").T @ mxq(hid, 0, "e4m3")

@@ -1,0 +1,320 @@
+from contextlib import ExitStack
+
+import concourse.mybir as mybir
+from concourse.masks import make_identity
+
+K, T, S, N, H, U = 512, 1024, 512, 128, 512, 1024
+FLOPS = 2 * K * H * S * 2 + 2 * H * N * U
+
+F32 = mybir.dt.float32
+BF16 = mybir.dt.bfloat16
+I32 = mybir.dt.int32
+U32 = mybir.dt.uint32
+U16 = mybir.dt.uint16
+U8 = mybir.dt.uint8
+FP8X4 = mybir.dt.float8_e4m3fn_x4
+ALU = mybir.AluOpType
+ACT = mybir.ActivationFunctionType
+
+P = 128
+PACK = 4
+GROUP = 4
+HALF = 512
+ROCK_WINDOW = S + 32
+FLUID_WINDOW = 2 * S
+CHUNKS = 8
+HID_BANKS = ((6, 7, 6, 7), (6, 7, 0, 2))
+OUT_BANKS = (6, 4)
+VECTOR_GATHERS = 4
+SPLIT_PAIRS = (2, 3,)
+ROOT10 = 10.0 ** 0.5
+TINY_LN = 2.0 ** -60
+TINY_ROOT = 1e-30
+
+
+def tile_picked_ygassm_imp_p_kernel(
+    tc, x_words, x_scales, w1, w2, por, rho, unit, w3, offs, rk, fl, out
+):
+    nc = tc.nc
+    with ExitStack() as ctx:
+        keep = ctx.enter_context(tc.tile_pool(name="keep", bufs=1))
+        work = ctx.enter_context(tc.tile_pool(name="work", bufs=2))
+        ring = ctx.enter_context(tc.tile_pool(name="ring", bufs=4))
+        psum = ctx.enter_context(tc.psum_pool(name="psum", bufs=1))
+
+        offs_t = keep.tile([P, S // 16], U16, name="offs_t")
+        rk_t = keep.tile([P, U // 16], U16, name="rk_t")
+        fl_t = keep.tile([P, U // 16], U16, name="fl_t")
+        xw = keep.tile([P, T], I32, name="xw", align_bytes=64)
+        xs = keep.tile([P, T], U8, name="xs", align_bytes=64)
+        nc.gpsimd.memset(xs[:], 0)
+        nc.sync.dma_start(offs_t[:], offs)
+        nc.sync.dma_start(xw[:], x_words[0].rearrange("p n t -> p (n t)").bitcast(I32))
+        for q in range(4):
+            nc.sync.dma_start(
+                xs[32 * q : 32 * q + 4, :].bitcast(I32), x_scales[0, 4 * q : 4 * q + 4, :].bitcast(I32)
+            )
+        w_raw = []
+        for name, w in (("w1_raw", w1), ("w2_raw", w2)):
+            raw = keep.tile([P, PACK, H], F32, name=name)
+            nc.sync.dma_start(raw[:], w.rearrange("(p j) c -> p j c", j=PACK))
+            w_raw.append(raw)
+        nc.sync.dma_start(rk_t[:], rk)
+        nc.sync.dma_start(fl_t[:], fl)
+        por_v = por.rearrange("(p t) r -> p t r", t=PACK)
+        rho_v = rho.rearrange("(p t) r -> p t r", t=PACK)
+        por_t = {}
+        rho_t = {}
+        unit_t = keep.tile([P, PACK], F32, name="unit_t")
+        w3_raw = keep.tile([P, PACK, N], F32, name="w3_raw")
+        for h in range(2):
+            for tp in range(2):
+                for name, view, tiles in (("por", por_v, por_t), ("rho", rho_v, rho_t)):
+                    tiles[h, tp] = keep.tile([P, 2, HALF], F32, name="%s%d%d" % (name, h, tp))
+                    nc.sync.dma_start(
+                        tiles[h, tp][:], view[:, 2 * tp : 2 * tp + 2, h * HALF : (h + 1) * HALF]
+                    )
+                if h == 0 and tp == 0:
+                    nc.sync.dma_start(unit_t[:], unit.rearrange("(p t) o -> p (t o)", t=PACK))
+                    nc.sync.dma_start(w3_raw[:], w3.rearrange("(p j) n -> p j n", j=PACK))
+
+        rock_win = [keep.tile([P, ROCK_WINDOW], F32, name="rock_win%d" % t) for t in range(PACK)]
+        fluid_win = [keep.tile([P, FLUID_WINDOW], F32, name="fluid_win%d" % t) for t in range(PACK)]
+        for win in rock_win + fluid_win:
+            nc.gpsimd.memset(win[:, S:], 0.0)
+        minus_one = keep.tile([P, 1], F32, name="minus_one")
+        nc.gpsimd.memset(minus_one[:], -1.0)
+        ident = keep.tile([P, P], F32, name="ident")
+        make_identity(nc, ident[:])
+
+        gw = keep.tile([P, S], U32, name="gw", align_bytes=64)
+        gs = keep.tile([P, S], U8, name="gs", align_bytes=64)
+        nc.vector.tensor_copy(gw[:], xw[:].bitcast(U32).indirect(offs_t[:]))
+        nc.vector.tensor_copy(gs[:], xs[:].indirect(offs_t[:]))
+
+        def bank(b):
+            return psum.tile([P, S], F32, name="bank%d" % b)
+
+        banks = [bank(b) for b in range(8)]
+        sig = keep.tile([P, 2, PACK, S], F32, name="sig")
+        for side in range(2):
+            wb = keep.tile([P, PACK, P, PACK], BF16, name="wb%d" % side, align_bytes=64)
+            nc.vector.tensor_copy(
+                wb[:].rearrange("p t m j -> p m j t"),
+                w_raw[side][:].rearrange("p j (m t) -> p m j t", t=PACK),
+            )
+            wq = keep.tile([P, H], U32, name="wq%d" % side, align_bytes=64)
+            ws = keep.tile([P, H], U8, name="ws%d" % side, align_bytes=64)
+            nc.vector.quantize_mx(
+                out=wq[:].bitcast(FP8X4), scales=ws[:], in_=wb[:].rearrange("p t m j -> p (t m j)")
+            )
+            for t in range(PACK):
+                nc.tensor.matmul_mx(
+                    out=banks[2 * t + side][:],
+                    lhsT=wq[:, t * P : (t + 1) * P].bitcast(FP8X4),
+                    lhsT_scale=ws[:, t * P : (t + 1) * P],
+                    rhs=gw[:].bitcast(FP8X4),
+                    rhs_scale=gs[:],
+                    start=True,
+                    stop=True,
+                )
+                nc.scalar.activation(sig[:, side, t, :], banks[2 * t + side][:], ACT.Sigmoid, scale=-1.0)
+
+        sp_fluid = keep.tile([P, PACK, S], F32, name="sp_fluid", tag="fluid")
+        for t in range(PACK):
+            nc.scalar.activation(sig[:, :, t, :], sig[:, :, t, :], ACT.Ln, bias=TINY_LN)
+            nc.vector.scalar_tensor_tensor(
+                sp_fluid[:, t, :], sig[:, 1, t, :], -1.0, banks[2 * t + 1][:], ALU.mult, ALU.max
+            )
+            nc.vector.scalar_tensor_tensor(
+                sig[:, 0, t, :], sig[:, 0, t, :], -1.0, banks[2 * t][:], ALU.mult, ALU.max
+            )
+            nc.vector.tensor_scalar(rock_win[t][:, :S], sig[:, 0, t, :], 1.9, None, ALU.add)
+        for t in range(PACK):
+            nc.scalar.activation(fluid_win[t][:, :S], sp_fluid[:, t, :], ACT.Ln, scale=5.0, bias=TINY_LN)
+
+        w3b = keep.tile([P, N, PACK], BF16, name="w3b", align_bytes=64)
+        nc.vector.tensor_copy(w3b[:], w3_raw[:].rearrange("p j n -> p n j"))
+        w3q = keep.tile([P, N], U32, name="w3q", align_bytes=64)
+        w3s = keep.tile([P, N], U8, name="w3s", align_bytes=64)
+        nc.vector.quantize_mx(
+            out=w3q[:].bitcast(FP8X4), scales=w3s[:], in_=w3b[:].rearrange("p n j -> p (n j)")
+        )
+
+        cols = HALF // 16
+        pore = keep.tile([P, CHUNKS, HALF], F32, name="pore", tag="fluid")
+        held = {}
+        imp = {}
+        pairs = {}
+
+        def by_member(ap):
+            return ap.rearrange("p (g d) -> p g d", d=GROUP)
+
+        def fetch_fluid(c):
+            h, t = divmod(c, PACK)
+            nc.scalar.activation(
+                pore[:, c, :],
+                fluid_win[t][:].indirect(fl_t[:, h * cols : (h + 1) * cols]),
+                ACT.Sigmoid,
+                scale=minus_one[:],
+            )
+
+        def fraction(pr):
+            h, tp = divmod(pr, 2)
+            split = pr in SPLIT_PAIRS
+            a = ring.tile([P, 2, HALF], F32, name="a", bufs=2)
+            for e in range(2):
+                picked = rock_win[2 * tp + e][:].indirect(rk_t[:, h * cols : (h + 1) * cols])
+                if 2 * pr + e < VECTOR_GATHERS:
+                    nc.vector.tensor_copy(a[:, e, :], picked)
+                else:
+                    nc.scalar.activation(a[:, e, :], picked, ACT.Copy, scale=0.036 if split else 1.0)
+            af = a[:].rearrange("p e c -> p (e c)")
+            square = ring.tile([P, GROUP, 2 * P], F32, name="square", bufs=2)
+            dry = ring.tile([P, GROUP, 2 * P], F32, name="dry", bufs=2)
+            den = ring.tile([P, 2 * HALF], F32, name="den", bufs=2)
+            x = pore[:, 2 * pr : 2 * pr + 2, :].rearrange("p e c -> p (e c)")
+            nc.vector.scalar_tensor_tensor(
+                x, x, -0.03, por_t[h, tp][:].rearrange("p e c -> p (e c)"), ALU.add, ALU.mult
+            )
+            if split:
+                nc.scalar.activation(den[:], af, ACT.Square, scale=1.0 / 0.036)
+                nc.scalar.activation(
+                    square[:].rearrange("p d g -> p g d"), by_member(af), ACT.Square,
+                    scale=0.2 / 0.036 ** 0.5, bias=-0.015 * 0.036 ** 0.5,
+                )
+                nc.vector.scalar_tensor_tensor(den[:], x, 0.006, den[:], ALU.add, ALU.mult)
+                shift = -0.054
+            else:
+                nc.scalar.activation(
+                    square[:].rearrange("p d g -> p g d"), by_member(af), ACT.Square,
+                    scale=0.2 / ROOT10, bias=1.2 / ROOT10,
+                )
+                nc.vector.scalar_tensor_tensor(x, x, 0.006, af, ALU.add, ALU.mult)
+                nc.vector.scalar_tensor_tensor(den[:], x, 0.036, af, ALU.add, ALU.mult)
+                shift = -1.5
+            nc.vector.scalar_tensor_tensor(
+                dry[:].rearrange("p d g -> p g d"), by_member(af), shift, by_member(den[:]), ALU.add, ALU.mult
+            )
+            held[2 * pr] = held[2 * pr + 1] = (a, square, den, dry)
+
+        def turn(c):
+            h, t = divmod(c, PACK)
+            e = c % 2
+            split = c // 2 in SPLIT_PAIRS
+            a, square, den, dry = held[c]
+            num_b, den_b, rho_b = bank(c % 2), bank(2 + c % 2), bank(4 + c % 2)
+            rho_c = rho_t[h, t // 2][:, e, :]
+            den_c = den[:, e * HALF : (e + 1) * HALF]
+            for d in range(GROUP):
+                nc.tensor.transpose(rho_b[:, d * P : (d + 1) * P], by_member(rho_c)[:, :, d], ident[:])
+            for d in range(GROUP):
+                o = num_b[:, d * P : (d + 1) * P]
+                nc.tensor.matmul(o, square[:, d, e * P : (e + 1) * P], ident[:], start=True, stop=False, is_transpose=True)
+                nc.tensor.matmul(o, dry[:, d, e * P : (e + 1) * P], ident[:], start=False, stop=True, is_transpose=True)
+            for d in range(GROUP):
+                o = den_b[:, d * P : (d + 1) * P]
+                if split:
+                    nc.tensor.matmul(o, by_member(a[:, e, :])[:, :, d], ident[:], start=True, stop=False, is_transpose=True)
+                    nc.tensor.matmul(o, by_member(den_c)[:, :, d], ident[:], start=False, stop=True, is_transpose=True)
+                else:
+                    nc.tensor.transpose(o, by_member(den_c)[:, :, d], ident[:])
+            top = ring.tile([P, HALF], F32, name="top", bufs=4)
+            nc.scalar.activation(top[:], num_b[:], ACT.Abs, bias=0.036 * 0.143775 if split else 0.0)
+            nc.vector.tensor_tensor(top[:], rho_b[:], top[:], ALU.mult)
+            prod = ring.tile([P, HALF], F32, name="prod", bufs=4)
+            nc.vector.tensor_tensor(prod[:], den_b[:], top[:], ALU.mult)
+            held[c] = (top, prod)
+
+        def root(c):
+            h, t = divmod(c, PACK)
+            top, prod = held[c]
+            if t == 0:
+                imp[h] = work.tile([P, PACK, GROUP * P], F32, name="imp")
+                pairs[h] = work.tile([P, PACK, 2 * P], F32, name="pair")
+            nc.scalar.activation(
+                prod[:], prod[:], ACT.Abs_reciprocal_sqrt, scale=0.036 if c // 2 in SPLIT_PAIRS else 1.0, bias=TINY_ROOT
+            )
+            nc.vector.tensor_tensor(imp[h][:, t, :], top[:], prod[:], ALU.mult)
+
+        def means(h, lo, hi):
+            v = imp[h][:, lo:hi, :]
+            pair = pairs[h][:, lo:hi, :]
+            nc.vector.tensor_tensor(pair, v[:, :, : 2 * P], v[:, :, 2 * P :], ALU.add)
+            nc.scalar.activation(pair, pair, ACT.Copy, scale=-0.2)
+
+        hid_banks = {}
+
+        def spread(h, d, lo, hi):
+            if lo == 0:
+                hid_banks[h, d] = bank(HID_BANKS[h][d])
+            for t in range(lo, hi):
+                o = hid_banks[h, d][:, t * P : (t + 1) * P]
+                terms = (imp[h][:, t, d * P : (d + 1) * P], pairs[h][:, t, :P], pairs[h][:, t, P:])
+                for i, term in enumerate(terms):
+                    nc.tensor.matmul(o, term, ident[:], start=(i == 0), stop=(i == 2), is_transpose=True)
+
+        def finish(h, lo):
+            hid = work.tile([P, GROUP, P, PACK], BF16, name="hid", align_bytes=64)
+            for d in range(GROUP):
+                spread(h, d, lo, PACK)
+                nc.vector.tensor_tensor(
+                    hid[:, d, :, :],
+                    hid_banks[h, d][:].rearrange("p (t g) -> p g t", t=PACK),
+                    unit_t[:].unsqueeze(1).to_broadcast([P, P, PACK]),
+                    ALU.mult,
+                )
+            hq = work.tile([P, HALF], U32, name="hq", align_bytes=64)
+            hs = work.tile([P, HALF], U8, name="hs", align_bytes=64)
+            nc.vector.quantize_mx(
+                out=hq[:].bitcast(FP8X4), scales=hs[:], in_=hid[:].rearrange("p d g t -> p (d g t)")
+            )
+            acc = bank(OUT_BANKS[h])
+            nc.tensor.matmul_mx(
+                out=acc[:],
+                lhsT=w3q[:].bitcast(FP8X4),
+                lhsT_scale=w3s[:],
+                rhs=hq[:].bitcast(FP8X4),
+                rhs_scale=hs[:],
+                start=True,
+                stop=True,
+            )
+            res = work.tile([P, P, GROUP], F32, name="res")
+            nc.scalar.copy(res[:], acc[:].rearrange("p (d g) -> p g d", d=GROUP))
+            nc.sync.dma_start(out[:, h * HALF : (h + 1) * HALF], res[:].rearrange("p g d -> p (g d)"))
+
+        fetch_fluid(0)
+        fetch_fluid(1)
+        fraction(0)
+        fetch_fluid(2)
+        fetch_fluid(3)
+        fraction(1)
+        fetch_fluid(4)
+        fetch_fluid(5)
+        turn(0)
+        fetch_fluid(6)
+        fetch_fluid(7)
+        turn(1)
+        fraction(2)
+        root(0)
+        turn(2)
+        root(1)
+        turn(3)
+        fraction(3)
+        root(2)
+        turn(4)
+        root(3)
+        means(0, 0, 4)
+        finish(0, 0)
+        turn(5)
+        root(4)
+        turn(6)
+        root(5)
+        turn(7)
+        root(6)
+        means(1, 0, 3)
+        for d in range(GROUP):
+            spread(1, d, 0, 3)
+        root(7)
+        means(1, 3, 4)
+        finish(1, 3)

@@ -1,7 +1,6 @@
 from contextlib import ExitStack
 
 import concourse.mybir as mybir
-from concourse.masks import make_identity
 
 K, T, S, N, H, U = 512, 1024, 512, 128, 512, 1024
 FLOPS = 2 * K * H * S * 2 + 2 * H * N * U
@@ -19,15 +18,12 @@ ACT = mybir.ActivationFunctionType
 P = 128
 PACK = 4
 GROUP = 4
-HALF = 512
-ROCK_WINDOW = S + 32
-FLUID_WINDOW = 2 * S
-CHUNKS = 8
-HID_BANKS = ((6, 7, 6, 7), (6, 7, 0, 2))
-OUT_BANKS = (6, 4)
-VECTOR_GATHERS = 4
-SPLIT_PAIRS = (2, 3,)
-ROOT10 = 10.0 ** 0.5
+SPANS = ((0, 0, 512), (0, 512, 1024), (1, 0, 512), (1, 512, 1024), (2, 0, 512), (2, 512, 1024), (3, 0, 512), (3, 512, 1024),)
+PIECES = ((0, 256), (256, 512), (512, 768), (768, 1024))
+VECTOR_GATHERS = (0, 1, 2, 3)
+SHIFTED = (0, 1)
+WINDOW = S + 32
+SLICE = 512
 TINY_LN = 2.0 ** -60
 TINY_ROOT = 1e-30
 
@@ -67,25 +63,18 @@ def tile_picked_ygassm_imp_p_kernel(
         rho_t = {}
         unit_t = keep.tile([P, PACK], F32, name="unit_t")
         w3_raw = keep.tile([P, PACK, N], F32, name="w3_raw")
-        for h in range(2):
-            for tp in range(2):
-                for name, view, tiles in (("por", por_v, por_t), ("rho", rho_v, rho_t)):
-                    tiles[h, tp] = keep.tile([P, 2, HALF], F32, name="%s%d%d" % (name, h, tp))
-                    nc.sync.dma_start(
-                        tiles[h, tp][:], view[:, 2 * tp : 2 * tp + 2, h * HALF : (h + 1) * HALF]
-                    )
-                if h == 0 and tp == 0:
-                    nc.sync.dma_start(unit_t[:], unit.rearrange("(p t) o -> p (t o)", t=PACK))
-                    nc.sync.dma_start(w3_raw[:], w3.rearrange("(p j) n -> p j n", j=PACK))
+        for t in range(PACK):
+            for name, view, tiles in (("por", por_v, por_t), ("rho", rho_v, rho_t)):
+                tiles[t] = keep.tile([P, U], F32, name="%s%d" % (name, t))
+                nc.sync.dma_start(tiles[t][:], view[:, t, :])
+            if t == 0:
+                nc.sync.dma_start(unit_t[:], unit.rearrange("(p t) o -> p (t o)", t=PACK))
+                nc.sync.dma_start(w3_raw[:], w3.rearrange("(p j) n -> p j n", j=PACK))
 
-        rock_win = [keep.tile([P, ROCK_WINDOW], F32, name="rock_win%d" % t) for t in range(PACK)]
-        fluid_win = [keep.tile([P, FLUID_WINDOW], F32, name="fluid_win%d" % t) for t in range(PACK)]
+        rock_win = [keep.tile([P, WINDOW], F32, name="rock_win%d" % t) for t in range(PACK)]
+        fluid_win = [keep.tile([P, WINDOW], F32, name="fluid_win%d" % t) for t in range(PACK)]
         for win in rock_win + fluid_win:
             nc.gpsimd.memset(win[:, S:], 0.0)
-        minus_one = keep.tile([P, 1], F32, name="minus_one")
-        nc.gpsimd.memset(minus_one[:], -1.0)
-        ident = keep.tile([P, P], F32, name="ident")
-        make_identity(nc, ident[:])
 
         gw = keep.tile([P, S], U32, name="gw", align_bytes=64)
         gs = keep.tile([P, S], U8, name="gs", align_bytes=64)
@@ -120,158 +109,122 @@ def tile_picked_ygassm_imp_p_kernel(
                 )
                 nc.scalar.activation(sig[:, side, t, :], banks[2 * t + side][:], ACT.Sigmoid, scale=-1.0)
 
-        sp_fluid = keep.tile([P, PACK, S], F32, name="sp_fluid", tag="fluid")
-        for t in range(PACK):
+        sp_fluid = keep.tile([P, PACK, S], F32, name="sp_fluid")
+
+        def softplus(t):
             nc.scalar.activation(sig[:, :, t, :], sig[:, :, t, :], ACT.Ln, bias=TINY_LN)
             nc.vector.scalar_tensor_tensor(
                 sp_fluid[:, t, :], sig[:, 1, t, :], -1.0, banks[2 * t + 1][:], ALU.mult, ALU.max
             )
             nc.vector.scalar_tensor_tensor(
-                sig[:, 0, t, :], sig[:, 0, t, :], -1.0, banks[2 * t][:], ALU.mult, ALU.max
+                rock_win[t][:, :S], sig[:, 0, t, :], -1.0, banks[2 * t][:], ALU.mult, ALU.max
             )
-            nc.vector.tensor_scalar(rock_win[t][:, :S], sig[:, 0, t, :], 1.9, None, ALU.add)
-        for t in range(PACK):
-            nc.scalar.activation(fluid_win[t][:, :S], sp_fluid[:, t, :], ACT.Ln, scale=5.0, bias=TINY_LN)
+            if t in SHIFTED:
+                nc.vector.tensor_scalar(rock_win[t][:, :S], rock_win[t][:, :S], 1.9, None, ALU.add)
 
-        w3b = keep.tile([P, N, PACK], BF16, name="w3b", align_bytes=64)
-        nc.vector.tensor_copy(w3b[:], w3_raw[:].rearrange("p j n -> p n j"))
+        def inverse(t):
+            nc.scalar.activation(
+                sp_fluid[:, t, :], sp_fluid[:, t, :], ACT.Abs_reciprocal_sqrt, scale=0.5, bias=0.1
+            )
+            nc.scalar.activation(fluid_win[t][:, :S], sp_fluid[:, t, :], ACT.Square)
+
+        def last_weights():
+            sign = keep.tile([P, PACK], F32, name="sign")
+            nc.vector.tensor_scalar(sign[:], unit_t[:], 0.0, 2.0, ALU.is_ge, ALU.mult)
+            nc.vector.tensor_scalar(sign[:], sign[:], -1.0, None, ALU.add)
+            nc.vector.tensor_scalar(fifth[:], unit_t[:], 0.2, None, ALU.mult)
+            nc.vector.tensor_tensor(squared[:], unit_t[:], unit_t[:], ALU.mult)
+            nc.vector.tensor_scalar(shift[:], squared[:], -1.5, None, ALU.mult)
+            w3b = keep.tile([P, N, PACK], BF16, name="w3b", align_bytes=64)
+            nc.vector.tensor_tensor(
+                w3b[:],
+                w3_raw[:].rearrange("p j n -> p n j"),
+                sign[:].unsqueeze(1).to_broadcast([P, N, PACK]),
+                ALU.mult,
+            )
+            nc.vector.quantize_mx(
+                out=w3q[:].bitcast(FP8X4), scales=w3s[:], in_=w3b[:].rearrange("p n j -> p (n j)")
+            )
+
         w3q = keep.tile([P, N], U32, name="w3q", align_bytes=64)
         w3s = keep.tile([P, N], U8, name="w3s", align_bytes=64)
-        nc.vector.quantize_mx(
-            out=w3q[:].bitcast(FP8X4), scales=w3s[:], in_=w3b[:].rearrange("p n j -> p (n j)")
-        )
-
-        cols = HALF // 16
-        pore = keep.tile([P, CHUNKS, HALF], F32, name="pore", tag="fluid")
+        fifth = keep.tile([P, PACK], F32, name="fifth")
+        squared = keep.tile([P, PACK], F32, name="squared")
+        shift = keep.tile([P, PACK], F32, name="shift")
+        modulus = keep.tile([P, PACK, U], F32, name="modulus")
         held = {}
-        imp = {}
-        pairs = {}
 
-        def by_member(ap):
-            return ap.rearrange("p (g d) -> p g d", d=GROUP)
-
-        def fetch_fluid(c):
-            h, t = divmod(c, PACK)
-            nc.scalar.activation(
-                pore[:, c, :],
-                fluid_win[t][:].indirect(fl_t[:, h * cols : (h + 1) * cols]),
-                ACT.Sigmoid,
-                scale=minus_one[:],
-            )
-
-        def fraction(pr):
-            h, tp = divmod(pr, 2)
-            split = pr in SPLIT_PAIRS
-            a = ring.tile([P, 2, HALF], F32, name="a", bufs=2)
-            for e in range(2):
-                picked = rock_win[2 * tp + e][:].indirect(rk_t[:, h * cols : (h + 1) * cols])
-                if 2 * pr + e < VECTOR_GATHERS:
-                    nc.vector.tensor_copy(a[:, e, :], picked)
-                else:
-                    nc.scalar.activation(a[:, e, :], picked, ACT.Copy, scale=0.036 if split else 1.0)
-            af = a[:].rearrange("p e c -> p (e c)")
-            square = ring.tile([P, GROUP, 2 * P], F32, name="square", bufs=2)
-            dry = ring.tile([P, GROUP, 2 * P], F32, name="dry", bufs=2)
-            den = ring.tile([P, 2 * HALF], F32, name="den", bufs=2)
-            x = pore[:, 2 * pr : 2 * pr + 2, :].rearrange("p e c -> p (e c)")
-            nc.vector.scalar_tensor_tensor(
-                x, x, -0.03, por_t[h, tp][:].rearrange("p e c -> p (e c)"), ALU.add, ALU.mult
-            )
-            if split:
-                nc.scalar.activation(den[:], af, ACT.Square, scale=1.0 / 0.036)
+        def fetch(i):
+            t, lo, hi = SPANS[i]
+            a = ring.tile([P, hi - lo], F32, name="a")
+            x = ring.tile([P, hi - lo], F32, name="x")
+            for c in range(lo, hi, SLICE):
                 nc.scalar.activation(
-                    square[:].rearrange("p d g -> p g d"), by_member(af), ACT.Square,
-                    scale=0.2 / 0.036 ** 0.5, bias=-0.015 * 0.036 ** 0.5,
+                    x[:, c - lo : c - lo + SLICE], fluid_win[t][:].indirect(fl_t[:, c // 16 : (c + SLICE) // 16]), ACT.Copy
                 )
-                nc.vector.scalar_tensor_tensor(den[:], x, 0.006, den[:], ALU.add, ALU.mult)
-                shift = -0.054
-            else:
-                nc.scalar.activation(
-                    square[:].rearrange("p d g -> p g d"), by_member(af), ACT.Square,
-                    scale=0.2 / ROOT10, bias=1.2 / ROOT10,
-                )
-                nc.vector.scalar_tensor_tensor(x, x, 0.006, af, ALU.add, ALU.mult)
-                nc.vector.scalar_tensor_tensor(den[:], x, 0.036, af, ALU.add, ALU.mult)
-                shift = -1.5
-            nc.vector.scalar_tensor_tensor(
-                dry[:].rearrange("p d g -> p g d"), by_member(af), shift, by_member(den[:]), ALU.add, ALU.mult
-            )
-            held[2 * pr] = held[2 * pr + 1] = (a, square, den, dry)
-
-        def turn(c):
-            h, t = divmod(c, PACK)
-            e = c % 2
-            split = c // 2 in SPLIT_PAIRS
-            a, square, den, dry = held[c]
-            num_b, den_b, rho_b = bank(c % 2), bank(2 + c % 2), bank(4 + c % 2)
-            rho_c = rho_t[h, t // 2][:, e, :]
-            den_c = den[:, e * HALF : (e + 1) * HALF]
-            for d in range(GROUP):
-                nc.tensor.transpose(rho_b[:, d * P : (d + 1) * P], by_member(rho_c)[:, :, d], ident[:])
-            for d in range(GROUP):
-                o = num_b[:, d * P : (d + 1) * P]
-                nc.tensor.matmul(o, square[:, d, e * P : (e + 1) * P], ident[:], start=True, stop=False, is_transpose=True)
-                nc.tensor.matmul(o, dry[:, d, e * P : (e + 1) * P], ident[:], start=False, stop=True, is_transpose=True)
-            for d in range(GROUP):
-                o = den_b[:, d * P : (d + 1) * P]
-                if split:
-                    nc.tensor.matmul(o, by_member(a[:, e, :])[:, :, d], ident[:], start=True, stop=False, is_transpose=True)
-                    nc.tensor.matmul(o, by_member(den_c)[:, :, d], ident[:], start=False, stop=True, is_transpose=True)
+            for c in range(lo, hi, SLICE):
+                picked = rock_win[t][:].indirect(rk_t[:, c // 16 : (c + SLICE) // 16])
+                if i in VECTOR_GATHERS:
+                    nc.vector.tensor_copy(a[:, c - lo : c - lo + SLICE], picked)
                 else:
-                    nc.tensor.transpose(o, by_member(den_c)[:, :, d], ident[:])
-            top = ring.tile([P, HALF], F32, name="top", bufs=4)
-            nc.scalar.activation(top[:], num_b[:], ACT.Abs, bias=0.036 * 0.143775 if split else 0.0)
-            nc.vector.tensor_tensor(top[:], rho_b[:], top[:], ALU.mult)
-            prod = ring.tile([P, HALF], F32, name="prod", bufs=4)
-            nc.vector.tensor_tensor(prod[:], den_b[:], top[:], ALU.mult)
-            held[c] = (top, prod)
+                    nc.scalar.activation(a[:, c - lo : c - lo + SLICE], picked, ACT.Copy, bias=0.0 if t in SHIFTED else 1.9)
+            held[i] = (a, x)
 
-        def root(c):
-            h, t = divmod(c, PACK)
-            top, prod = held[c]
-            if t == 0:
-                imp[h] = work.tile([P, PACK, GROUP * P], F32, name="imp")
-                pairs[h] = work.tile([P, PACK, 2 * P], F32, name="pair")
-            nc.scalar.activation(
-                prod[:], prod[:], ACT.Abs_reciprocal_sqrt, scale=0.036 if c // 2 in SPLIT_PAIRS else 1.0, bias=TINY_ROOT
+        def denominator(i):
+            t, lo, hi = SPANS[i]
+            a, x = held[i]
+            nc.vector.scalar_tensor_tensor(x[:], x[:], -0.3, por_t[t][:, lo:hi], ALU.add, ALU.mult)
+            nc.vector.scalar_tensor_tensor(x[:], x[:], 0.06, a[:], ALU.add, ALU.mult)
+            nc.vector.scalar_tensor_tensor(x[:], x[:], 0.36, a[:], ALU.add, ALU.mult)
+            y = ring.tile([P, hi - lo], F32, name="y")
+            nc.scalar.activation(y[:], x[:], ACT.Abs_reciprocal_sqrt, bias=TINY_ROOT)
+            nc.scalar.activation(x[:], x[:], ACT.Sign)
+            held[i] = (a, x, y)
+
+        def quotient(i):
+            t = SPANS[i][0]
+            a, x, y = held[i]
+            nc.vector.scalar_tensor_tensor(y[:], a[:], 6.0, y[:], ALU.add, ALU.mult)
+            nc.scalar.activation(y[:], y[:], ACT.Square, scale=fifth[:, t : t + 1])
+
+        def saturate(i):
+            t, lo, hi = SPANS[i]
+            a, x, y = held[i]
+            nc.vector.tensor_tensor(y[:], y[:], x[:], ALU.mult)
+            nc.vector.scalar_tensor_tensor(y[:], a[:], squared[:, t : t + 1], y[:], ALU.mult, ALU.add)
+            nc.vector.scalar_tensor_tensor(
+                modulus[:, t, lo:hi], y[:], shift[:, t : t + 1], rho_t[t][:, lo:hi], ALU.add, ALU.mult
             )
-            nc.vector.tensor_tensor(imp[h][:, t, :], top[:], prod[:], ALU.mult)
 
-        def means(h, lo, hi):
-            v = imp[h][:, lo:hi, :]
-            pair = pairs[h][:, lo:hi, :]
-            nc.vector.tensor_tensor(pair, v[:, :, : 2 * P], v[:, :, 2 * P :], ALU.add)
-            nc.scalar.activation(pair, pair, ACT.Copy, scale=-0.2)
+        def weave(h):
+            lo, hi = PIECES[h]
+            imp = keep.tile([P, GROUP, (hi - lo) // GROUP, PACK], F32, name="imp%d" % h)
+            nc.scalar.activation(
+                imp[:].rearrange("p d g t -> p g t d"),
+                modulus[:, :, lo:hi].rearrange("p t (g d) -> p g t d", d=GROUP),
+                ACT.Sqrt,
+            )
+            held["imp", h] = imp
 
-        hid_banks = {}
-
-        def spread(h, d, lo, hi):
-            if lo == 0:
-                hid_banks[h, d] = bank(HID_BANKS[h][d])
-            for t in range(lo, hi):
-                o = hid_banks[h, d][:, t * P : (t + 1) * P]
-                terms = (imp[h][:, t, d * P : (d + 1) * P], pairs[h][:, t, :P], pairs[h][:, t, P:])
-                for i, term in enumerate(terms):
-                    nc.tensor.matmul(o, term, ident[:], start=(i == 0), stop=(i == 2), is_transpose=True)
-
-        def finish(h, lo):
-            hid = work.tile([P, GROUP, P, PACK], BF16, name="hid", align_bytes=64)
-            for d in range(GROUP):
-                spread(h, d, lo, PACK)
-                nc.vector.tensor_tensor(
-                    hid[:, d, :, :],
-                    hid_banks[h, d][:].rearrange("p (t g) -> p g t", t=PACK),
-                    unit_t[:].unsqueeze(1).to_broadcast([P, P, PACK]),
-                    ALU.mult,
-                )
-            hq = work.tile([P, HALF], U32, name="hq", align_bytes=64)
-            hs = work.tile([P, HALF], U8, name="hs", align_bytes=64)
+        def finish(h):
+            lo, hi = PIECES[h]
+            width = hi - lo
+            impf = held["imp", h][:].rearrange("p d g t -> p d (g t)")
+            pair = work.tile([P, 2, width], F32, name="pair")
+            nc.vector.tensor_tensor(pair[:], impf[:, 0:2, :], impf[:, 2:4, :], ALU.add)
+            nc.vector.tensor_tensor(pair[:, 0, :], pair[:, 0, :], pair[:, 1, :], ALU.add)
+            hid = work.tile([P, GROUP, width], BF16, name="hid", align_bytes=64)
+            nc.vector.scalar_tensor_tensor(
+                hid[:], pair[:, 0:1, :].to_broadcast([P, GROUP, width]), -0.2, impf, ALU.mult, ALU.add
+            )
+            hq = work.tile([P, width], U32, name="hq", align_bytes=64)
+            hs = work.tile([P, width], U8, name="hs", align_bytes=64)
             nc.vector.quantize_mx(
-                out=hq[:].bitcast(FP8X4), scales=hs[:], in_=hid[:].rearrange("p d g t -> p (d g t)")
+                out=hq[:].bitcast(FP8X4), scales=hs[:], in_=hid[:].rearrange("p d c -> p (d c)")
             )
-            acc = bank(OUT_BANKS[h])
+            acc = bank(h % 2)
             nc.tensor.matmul_mx(
-                out=acc[:],
+                out=acc[:, :width],
                 lhsT=w3q[:].bitcast(FP8X4),
                 lhsT_scale=w3s[:],
                 rhs=hq[:].bitcast(FP8X4),
@@ -279,42 +232,56 @@ def tile_picked_ygassm_imp_p_kernel(
                 start=True,
                 stop=True,
             )
-            res = work.tile([P, P, GROUP], F32, name="res")
-            nc.scalar.copy(res[:], acc[:].rearrange("p (d g) -> p g d", d=GROUP))
-            nc.sync.dma_start(out[:, h * HALF : (h + 1) * HALF], res[:].rearrange("p g d -> p (g d)"))
+            res = work.tile([P, width // GROUP, GROUP], F32, name="res")
+            nc.scalar.copy(res[:], acc[:, :width].rearrange("p (d g) -> p g d", d=GROUP))
+            nc.sync.dma_start(out[:, lo:hi], res[:].rearrange("p g d -> p (g d)"))
 
-        fetch_fluid(0)
-        fetch_fluid(1)
-        fraction(0)
-        fetch_fluid(2)
-        fetch_fluid(3)
-        fraction(1)
-        fetch_fluid(4)
-        fetch_fluid(5)
-        turn(0)
-        fetch_fluid(6)
-        fetch_fluid(7)
-        turn(1)
-        fraction(2)
-        root(0)
-        turn(2)
-        root(1)
-        turn(3)
-        fraction(3)
-        root(2)
-        turn(4)
-        root(3)
-        means(0, 0, 4)
-        finish(0, 0)
-        turn(5)
-        root(4)
-        turn(6)
-        root(5)
-        turn(7)
-        root(6)
-        means(1, 0, 3)
-        for d in range(GROUP):
-            spread(1, d, 0, 3)
-        root(7)
-        means(1, 3, 4)
-        finish(1, 3)
+        last_weights()
+        softplus(0)
+        softplus(1)
+        softplus(2)
+        softplus(3)
+        inverse(0)
+        fetch(0)
+        inverse(1)
+        fetch(1)
+        denominator(0)
+        inverse(2)
+        fetch(2)
+        quotient(0)
+        denominator(1)
+        inverse(3)
+        fetch(3)
+        saturate(0)
+        quotient(1)
+        denominator(2)
+        fetch(4)
+        saturate(1)
+        quotient(2)
+        denominator(3)
+        fetch(5)
+        saturate(2)
+        quotient(3)
+        denominator(4)
+        fetch(6)
+        saturate(3)
+        quotient(4)
+        denominator(5)
+        fetch(7)
+        saturate(4)
+        quotient(5)
+        denominator(6)
+        saturate(5)
+        quotient(6)
+        denominator(7)
+        saturate(6)
+        quotient(7)
+        saturate(7)
+        weave(0)
+        weave(1)
+        weave(2)
+        weave(3)
+        finish(0)
+        finish(1)
+        finish(2)
+        finish(3)

@@ -18,9 +18,9 @@ ACT = mybir.ActivationFunctionType
 P = 128
 PACK = 4
 GROUP = 4
-SPANS = ((0, 0, 512), (0, 512, 1024), (1, 0, 512), (1, 512, 1024), (2, 0, 512), (2, 512, 1024), (3, 0, 512), (3, 512, 1024),)
+SPANS = ((0, 0, 512), (0, 512, 1024), (1, 0, 1024), (2, 0, 1024), (3, 0, 512), (3, 512, 1024),)
 PIECES = ((0, 256), (256, 512), (512, 768), (768, 1024))
-VECTOR_GATHERS = (0, 1, 2, 3)
+VECTOR_GATHERS = (0, 1, 2)
 SHIFTED = (0, 1)
 WINDOW = S + 32
 SLICE = 512
@@ -35,7 +35,7 @@ def tile_picked_ygassm_imp_p_kernel(
     with ExitStack() as ctx:
         keep = ctx.enter_context(tc.tile_pool(name="keep", bufs=1))
         work = ctx.enter_context(tc.tile_pool(name="work", bufs=2))
-        ring = ctx.enter_context(tc.tile_pool(name="ring", bufs=4))
+        ring = ctx.enter_context(tc.tile_pool(name="ring", bufs=3))
         psum = ctx.enter_context(tc.psum_pool(name="psum", bufs=1))
 
         offs_t = keep.tile([P, S // 16], U16, name="offs_t")
@@ -43,7 +43,7 @@ def tile_picked_ygassm_imp_p_kernel(
         fl_t = keep.tile([P, U // 16], U16, name="fl_t")
         xw = keep.tile([P, T], I32, name="xw", align_bytes=64)
         xs = keep.tile([P, T], U8, name="xs", align_bytes=64)
-        nc.gpsimd.memset(xs[:], 0)
+        nc.gpsimd.memset(xs[:].bitcast(I32), 0)
         nc.sync.dma_start(offs_t[:], offs)
         nc.sync.dma_start(xw[:], x_words[0].rearrange("p n t -> p (n t)").bitcast(I32))
         for q in range(4):
@@ -263,20 +263,12 @@ def tile_picked_ygassm_imp_p_kernel(
         saturate(2)
         quotient(3)
         denominator(4)
-        fetch(6)
         saturate(3)
         quotient(4)
         denominator(5)
-        fetch(7)
         saturate(4)
         quotient(5)
-        denominator(6)
         saturate(5)
-        quotient(6)
-        denominator(7)
-        saturate(6)
-        quotient(7)
-        saturate(7)
         weave(0)
         weave(1)
         weave(2)

@@ -94,10 +94,12 @@ def tile_picked_ygassm_imp_p_kernel(
             )
             wq = keep.tile([P, H], U32, name="wq%d" % side, align_bytes=64)
             ws = keep.tile([P, H], U8, name="ws%d" % side, align_bytes=64)
-            nc.vector.quantize_mx(
-                out=wq[:].bitcast(FP8X4), scales=ws[:], in_=wb[:].rearrange("p t m j -> p (t m j)")
-            )
             for t in range(PACK):
+                nc.vector.quantize_mx(
+                    out=wq[:, t * P : (t + 1) * P].bitcast(FP8X4),
+                    scales=ws[:, t * P : (t + 1) * P],
+                    in_=wb[:, t].rearrange("p m j -> p (m j)"),
+                )
                 nc.tensor.matmul_mx(
                     out=banks[2 * t + side][:],
                     lhsT=wq[:, t * P : (t + 1) * P].bitcast(FP8X4),
@@ -120,13 +122,13 @@ def tile_picked_ygassm_imp_p_kernel(
                 rock_win[t][:, :S], sig[:, 0, t, :], -1.0, banks[2 * t][:], ALU.mult, ALU.max
             )
             if t in SHIFTED:
-                nc.vector.tensor_scalar(rock_win[t][:, :S], rock_win[t][:, :S], 1.9, None, ALU.add)
+                nc.gpsimd.tensor_scalar(rock_win[t][:, :S], rock_win[t][:, :S], 1.0, 1.9, ALU.mult, ALU.add)
 
         def inverse(t):
             nc.scalar.activation(
                 sp_fluid[:, t, :], sp_fluid[:, t, :], ACT.Abs_reciprocal_sqrt, scale=0.5, bias=0.1
             )
-            nc.scalar.activation(fluid_win[t][:, :S], sp_fluid[:, t, :], ACT.Square)
+            nc.gpsimd.tensor_tensor(fluid_win[t][:, :S], sp_fluid[:, t, :], sp_fluid[:, t, :], ALU.mult)
 
         def last_weights():
             sign = keep.tile([P, PACK], F32, name="sign")

@@ -18,14 +18,22 @@ ACT = mybir.ActivationFunctionType
 P = 128
 PACK = 4
 GROUP = 4
-SPANS = ((0, 0, 512), (0, 512, 1024), (1, 0, 1024), (2, 0, 1024), (3, 0, 512), (3, 512, 1024),)
-PIECES = ((0, 256), (256, 512), (512, 768), (768, 1024))
-VECTOR_GATHERS = (0, 1, 2)
-SHIFTED = (0, 1)
-WINDOW = S + 32
+STRIPE = 16
+QUADRANT = 32
 SLICE = 512
-TINY_LN = 2.0 ** -60
-TINY_ROOT = 1e-30
+WINDOW = S + 32
+SPANS = tuple(
+    (t, lo, lo + width)
+    for t in range(PACK)
+    for width in [U // 2 if t in (0, PACK - 1) else U]
+    for lo in range(0, U, width)
+)
+VECTOR_TILES = 2
+PIECE = 256
+SPANS_IN_FLIGHT = 3
+ROCK_SHIFT = 0.4 + 1.5
+LN_FLOOR = 2.0**-60
+ROOT_FLOOR = 1e-30
 
 
 def tile_picked_ygassm_imp_p_kernel(
@@ -35,20 +43,21 @@ def tile_picked_ygassm_imp_p_kernel(
     with ExitStack() as ctx:
         keep = ctx.enter_context(tc.tile_pool(name="keep", bufs=1))
         work = ctx.enter_context(tc.tile_pool(name="work", bufs=2))
-        ring = ctx.enter_context(tc.tile_pool(name="ring", bufs=3))
+        ring = ctx.enter_context(tc.tile_pool(name="ring", bufs=SPANS_IN_FLIGHT))
         psum = ctx.enter_context(tc.psum_pool(name="psum", bufs=1))
 
-        offs_t = keep.tile([P, S // 16], U16, name="offs_t")
-        rk_t = keep.tile([P, U // 16], U16, name="rk_t")
-        fl_t = keep.tile([P, U // 16], U16, name="fl_t")
+        offs_t = keep.tile([P, S // STRIPE], U16, name="offs_t")
+        rk_t = keep.tile([P, U // STRIPE], U16, name="rk_t")
+        fl_t = keep.tile([P, U // STRIPE], U16, name="fl_t")
         xw = keep.tile([P, T], I32, name="xw", align_bytes=64)
         xs = keep.tile([P, T], U8, name="xs", align_bytes=64)
         nc.gpsimd.memset(xs[:].bitcast(I32), 0)
         nc.sync.dma_start(offs_t[:], offs)
         nc.sync.dma_start(xw[:], x_words[0].rearrange("p n t -> p (n t)").bitcast(I32))
-        for q in range(4):
+        for q in range(P // QUADRANT):
             nc.sync.dma_start(
-                xs[32 * q : 32 * q + 4, :].bitcast(I32), x_scales[0, 4 * q : 4 * q + 4, :].bitcast(I32)
+                xs[QUADRANT * q : QUADRANT * q + 4, :].bitcast(I32),
+                x_scales[0, 4 * q : 4 * q + 4, :].bitcast(I32),
             )
         w_raw = []
         for name, w in (("w1_raw", w1), ("w2_raw", w2)):
@@ -84,7 +93,7 @@ def tile_picked_ygassm_imp_p_kernel(
         def bank(b):
             return psum.tile([P, S], F32, name="bank%d" % b)
 
-        banks = [bank(b) for b in range(8)]
+        banks = [bank(b) for b in range(2 * PACK)]
         sig = keep.tile([P, 2, PACK, S], F32, name="sig")
         for side in range(2):
             wb = keep.tile([P, PACK, P, PACK], BF16, name="wb%d" % side, align_bytes=64)
@@ -111,122 +120,117 @@ def tile_picked_ygassm_imp_p_kernel(
                 )
                 nc.scalar.activation(sig[:, side, t, :], banks[2 * t + side][:], ACT.Sigmoid, scale=-1.0)
 
-        sp_fluid = keep.tile([P, PACK, S], F32, name="sp_fluid")
+        fluid = keep.tile([P, PACK, S], F32, name="sp_fluid")
 
         def softplus(t):
-            nc.scalar.activation(sig[:, :, t, :], sig[:, :, t, :], ACT.Ln, bias=TINY_LN)
+            nc.scalar.activation(sig[:, :, t, :], sig[:, :, t, :], ACT.Ln, bias=LN_FLOOR)
             nc.vector.scalar_tensor_tensor(
-                sp_fluid[:, t, :], sig[:, 1, t, :], -1.0, banks[2 * t + 1][:], ALU.mult, ALU.max
+                fluid[:, t, :], sig[:, 1, t, :], -1.0, banks[2 * t + 1][:], ALU.mult, ALU.max
             )
             nc.vector.scalar_tensor_tensor(
                 rock_win[t][:, :S], sig[:, 0, t, :], -1.0, banks[2 * t][:], ALU.mult, ALU.max
             )
-            if t in SHIFTED:
-                nc.gpsimd.tensor_scalar(rock_win[t][:, :S], rock_win[t][:, :S], 1.0, 1.9, ALU.mult, ALU.add)
+            if t < VECTOR_TILES:
+                nc.gpsimd.tensor_scalar(rock_win[t][:, :S], rock_win[t][:, :S], 1.0, ROCK_SHIFT, ALU.mult, ALU.add)
 
-        def inverse(t):
-            nc.scalar.activation(
-                sp_fluid[:, t, :], sp_fluid[:, t, :], ACT.Abs_reciprocal_sqrt, scale=0.5, bias=0.1
-            )
-            nc.gpsimd.tensor_tensor(fluid_win[t][:, :S], sp_fluid[:, t, :], sp_fluid[:, t, :], ALU.mult)
+        def invert_fluid(t):
+            nc.scalar.activation(fluid[:, t, :], fluid[:, t, :], ACT.Abs_reciprocal_sqrt, scale=0.5, bias=0.1)
+            nc.gpsimd.tensor_tensor(fluid_win[t][:, :S], fluid[:, t, :], fluid[:, t, :], ALU.mult)
 
-        def last_weights():
-            sign = keep.tile([P, PACK], F32, name="sign")
-            nc.vector.tensor_scalar(sign[:], unit_t[:], 0.0, 2.0, ALU.is_ge, ALU.mult)
-            nc.vector.tensor_scalar(sign[:], sign[:], -1.0, None, ALU.add)
-            nc.vector.tensor_scalar(fifth[:], unit_t[:], 0.2, None, ALU.mult)
-            nc.vector.tensor_tensor(squared[:], unit_t[:], unit_t[:], ALU.mult)
-            nc.vector.tensor_scalar(shift[:], squared[:], -1.5, None, ALU.mult)
+        w3q = keep.tile([P, N], U32, name="w3q", align_bytes=64)
+        w3s = keep.tile([P, N], U8, name="w3s", align_bytes=64)
+        unit_fifth = keep.tile([P, PACK], F32, name="fifth")
+        unit_squared = keep.tile([P, PACK], F32, name="squared")
+        unit_shift = keep.tile([P, PACK], F32, name="shift")
+        modulus = keep.tile([P, PACK, U], F32, name="modulus")
+        span_tiles = {}
+        woven = {}
+
+        def prepare_unit_and_w3():
+            unit_sign = keep.tile([P, PACK], F32, name="sign")
+            nc.vector.tensor_scalar(unit_sign[:], unit_t[:], 0.0, 2.0, ALU.is_ge, ALU.mult)
+            nc.vector.tensor_scalar(unit_sign[:], unit_sign[:], -1.0, None, ALU.add)
+            nc.vector.tensor_scalar(unit_fifth[:], unit_t[:], 0.2, None, ALU.mult)
+            nc.vector.tensor_tensor(unit_squared[:], unit_t[:], unit_t[:], ALU.mult)
+            nc.vector.tensor_scalar(unit_shift[:], unit_squared[:], -1.5, None, ALU.mult)
             w3b = keep.tile([P, N, PACK], BF16, name="w3b", align_bytes=64)
             nc.vector.tensor_tensor(
                 w3b[:],
                 w3_raw[:].rearrange("p j n -> p n j"),
-                sign[:].unsqueeze(1).to_broadcast([P, N, PACK]),
+                unit_sign[:].unsqueeze(1).to_broadcast([P, N, PACK]),
                 ALU.mult,
             )
             nc.vector.quantize_mx(
                 out=w3q[:].bitcast(FP8X4), scales=w3s[:], in_=w3b[:].rearrange("p n j -> p (n j)")
             )
 
-        w3q = keep.tile([P, N], U32, name="w3q", align_bytes=64)
-        w3s = keep.tile([P, N], U8, name="w3s", align_bytes=64)
-        fifth = keep.tile([P, PACK], F32, name="fifth")
-        squared = keep.tile([P, PACK], F32, name="squared")
-        shift = keep.tile([P, PACK], F32, name="shift")
-        modulus = keep.tile([P, PACK, U], F32, name="modulus")
-        held = {}
-
         def fetch(i):
             t, lo, hi = SPANS[i]
             a = ring.tile([P, hi - lo], F32, name="a")
-            x = ring.tile([P, hi - lo], F32, name="x")
+            den = ring.tile([P, hi - lo], F32, name="x")
             for c in range(lo, hi, SLICE):
-                nc.scalar.activation(
-                    x[:, c - lo : c - lo + SLICE], fluid_win[t][:].indirect(fl_t[:, c // 16 : (c + SLICE) // 16]), ACT.Copy
-                )
+                picked = fluid_win[t][:].indirect(fl_t[:, c // STRIPE : (c + SLICE) // STRIPE])
+                nc.scalar.activation(den[:, c - lo : c - lo + SLICE], picked, ACT.Copy)
             for c in range(lo, hi, SLICE):
-                picked = rock_win[t][:].indirect(rk_t[:, c // 16 : (c + SLICE) // 16])
-                if i in VECTOR_GATHERS:
+                picked = rock_win[t][:].indirect(rk_t[:, c // STRIPE : (c + SLICE) // STRIPE])
+                if t < VECTOR_TILES:
                     nc.vector.tensor_copy(a[:, c - lo : c - lo + SLICE], picked)
                 else:
-                    nc.scalar.activation(a[:, c - lo : c - lo + SLICE], picked, ACT.Copy, bias=0.0 if t in SHIFTED else 1.9)
-            held[i] = (a, x)
+                    nc.scalar.activation(a[:, c - lo : c - lo + SLICE], picked, ACT.Copy, bias=ROCK_SHIFT)
+            span_tiles[i] = (a, den)
 
         def denominator(i):
             t, lo, hi = SPANS[i]
-            a, x = held[i]
-            nc.vector.scalar_tensor_tensor(x[:], x[:], -0.3, por_t[t][:, lo:hi], ALU.add, ALU.mult)
-            nc.vector.scalar_tensor_tensor(x[:], x[:], 0.06, a[:], ALU.add, ALU.mult)
-            nc.vector.scalar_tensor_tensor(x[:], x[:], 0.36, a[:], ALU.add, ALU.mult)
-            y = ring.tile([P, hi - lo], F32, name="y")
-            nc.scalar.activation(y[:], x[:], ACT.Abs_reciprocal_sqrt, bias=TINY_ROOT)
-            nc.scalar.activation(x[:], x[:], ACT.Sign)
-            held[i] = (a, x, y)
+            a, den = span_tiles[i]
+            nc.vector.scalar_tensor_tensor(den[:], den[:], -0.3, por_t[t][:, lo:hi], ALU.add, ALU.mult)
+            nc.vector.scalar_tensor_tensor(den[:], den[:], 0.06, a[:], ALU.add, ALU.mult)
+            nc.vector.scalar_tensor_tensor(den[:], den[:], 0.36, a[:], ALU.add, ALU.mult)
+            term = ring.tile([P, hi - lo], F32, name="y")
+            nc.scalar.activation(term[:], den[:], ACT.Abs_reciprocal_sqrt, bias=ROOT_FLOOR)
+            nc.scalar.activation(den[:], den[:], ACT.Sign)
+            span_tiles[i] = (a, den, term)
 
         def quotient(i):
             t = SPANS[i][0]
-            a, x, y = held[i]
-            nc.vector.scalar_tensor_tensor(y[:], a[:], 6.0, y[:], ALU.add, ALU.mult)
-            nc.scalar.activation(y[:], y[:], ACT.Square, scale=fifth[:, t : t + 1])
+            a, den_sign, term = span_tiles[i]
+            nc.vector.scalar_tensor_tensor(term[:], a[:], 6.0, term[:], ALU.add, ALU.mult)
+            nc.scalar.activation(term[:], term[:], ACT.Square, scale=unit_fifth[:, t : t + 1])
 
         def saturate(i):
             t, lo, hi = SPANS[i]
-            a, x, y = held[i]
-            nc.vector.tensor_tensor(y[:], y[:], x[:], ALU.mult)
-            nc.vector.scalar_tensor_tensor(y[:], a[:], squared[:, t : t + 1], y[:], ALU.mult, ALU.add)
+            a, den_sign, term = span_tiles[i]
+            nc.vector.tensor_tensor(term[:], term[:], den_sign[:], ALU.mult)
+            nc.vector.scalar_tensor_tensor(term[:], a[:], unit_squared[:, t : t + 1], term[:], ALU.mult, ALU.add)
             nc.vector.scalar_tensor_tensor(
-                modulus[:, t, lo:hi], y[:], shift[:, t : t + 1], rho_t[t][:, lo:hi], ALU.add, ALU.mult
+                modulus[:, t, lo:hi], term[:], unit_shift[:, t : t + 1], rho_t[t][:, lo:hi], ALU.add, ALU.mult
             )
 
         def weave(h):
-            lo, hi = PIECES[h]
-            imp = keep.tile([P, GROUP, (hi - lo) // GROUP, PACK], F32, name="imp%d" % h)
+            imp = keep.tile([P, GROUP, PIECE // GROUP, PACK], F32, name="imp%d" % h)
             nc.scalar.activation(
                 imp[:].rearrange("p d g t -> p g t d"),
-                modulus[:, :, lo:hi].rearrange("p t (g d) -> p g t d", d=GROUP),
+                modulus[:, :, h * PIECE : (h + 1) * PIECE].rearrange("p t (g d) -> p g t d", d=GROUP),
                 ACT.Sqrt,
             )
-            held["imp", h] = imp
+            woven[h] = imp
 
         def finish(h):
-            lo, hi = PIECES[h]
-            width = hi - lo
-            impf = held["imp", h][:].rearrange("p d g t -> p d (g t)")
-            pair = work.tile([P, 2, width], F32, name="pair")
-            nc.vector.tensor_tensor(pair[:], impf[:, 0:2, :], impf[:, 2:4, :], ALU.add)
-            nc.vector.tensor_tensor(pair[:, 0, :], pair[:, 0, :], pair[:, 1, :], ALU.add)
-            hid = work.tile([P, GROUP, width], BF16, name="hid", align_bytes=64)
+            members = woven[h][:].rearrange("p d g t -> p d (g t)")
+            sums = work.tile([P, 2, PIECE], F32, name="pair")
+            nc.vector.tensor_tensor(sums[:], members[:, 0:2, :], members[:, 2:4, :], ALU.add)
+            nc.vector.tensor_tensor(sums[:, 0, :], sums[:, 0, :], sums[:, 1, :], ALU.add)
+            hid = work.tile([P, GROUP, PIECE], BF16, name="hid", align_bytes=64)
             nc.vector.scalar_tensor_tensor(
-                hid[:], pair[:, 0:1, :].to_broadcast([P, GROUP, width]), -0.2, impf, ALU.mult, ALU.add
+                hid[:], sums[:, 0:1, :].to_broadcast([P, GROUP, PIECE]), -0.2, members, ALU.mult, ALU.add
             )
-            hq = work.tile([P, width], U32, name="hq", align_bytes=64)
-            hs = work.tile([P, width], U8, name="hs", align_bytes=64)
+            hq = work.tile([P, PIECE], U32, name="hq", align_bytes=64)
+            hs = work.tile([P, PIECE], U8, name="hs", align_bytes=64)
             nc.vector.quantize_mx(
                 out=hq[:].bitcast(FP8X4), scales=hs[:], in_=hid[:].rearrange("p d c -> p (d c)")
             )
             acc = bank(h % 2)
             nc.tensor.matmul_mx(
-                out=acc[:, :width],
+                out=acc[:, :PIECE],
                 lhsT=w3q[:].bitcast(FP8X4),
                 lhsT_scale=w3s[:],
                 rhs=hq[:].bitcast(FP8X4),
@@ -234,48 +238,20 @@ def tile_picked_ygassm_imp_p_kernel(
                 start=True,
                 stop=True,
             )
-            res = work.tile([P, width // GROUP, GROUP], F32, name="res")
-            nc.scalar.copy(res[:], acc[:, :width].rearrange("p (d g) -> p g d", d=GROUP))
-            nc.sync.dma_start(out[:, lo:hi], res[:].rearrange("p g d -> p (g d)"))
+            res = work.tile([P, PIECE // GROUP, GROUP], F32, name="res")
+            nc.scalar.copy(res[:], acc[:, :PIECE].rearrange("p (d g) -> p g d", d=GROUP))
+            nc.sync.dma_start(out[:, h * PIECE : (h + 1) * PIECE], res[:].rearrange("p g d -> p (g d)"))
 
-        last_weights()
-        softplus(0)
-        softplus(1)
-        softplus(2)
-        softplus(3)
-        inverse(0)
-        fetch(0)
-        inverse(1)
-        fetch(1)
-        denominator(0)
-        inverse(2)
-        fetch(2)
-        quotient(0)
-        denominator(1)
-        inverse(3)
-        fetch(3)
-        saturate(0)
-        quotient(1)
-        denominator(2)
-        fetch(4)
-        saturate(1)
-        quotient(2)
-        denominator(3)
-        fetch(5)
-        saturate(2)
-        quotient(3)
-        denominator(4)
-        saturate(3)
-        quotient(4)
-        denominator(5)
-        saturate(4)
-        quotient(5)
-        saturate(5)
-        weave(0)
-        weave(1)
-        weave(2)
-        weave(3)
-        finish(0)
-        finish(1)
-        finish(2)
-        finish(3)
+        prepare_unit_and_w3()
+        for t in range(PACK):
+            softplus(t)
+        for t in range(PACK):
+            invert_fluid(t)
+        for step in range(len(SPANS) + 3):
+            for stage, lag in ((fetch, 0), (saturate, 3), (quotient, 2), (denominator, 1)):
+                if 0 <= step - lag < len(SPANS):
+                    stage(step - lag)
+        for h in range(U // PIECE):
+            weave(h)
+        for h in range(U // PIECE):
+            finish(h)

from contextlib import ExitStack

import concourse.mybir as mybir

K, T, S, N, H, U = 512, 1024, 512, 128, 512, 1024
FLOPS = 2 * K * H * S * 2 + 2 * H * N * U

F32 = mybir.dt.float32
BF16 = mybir.dt.bfloat16
I32 = mybir.dt.int32
U32 = mybir.dt.uint32
U16 = mybir.dt.uint16
U8 = mybir.dt.uint8
FP8X4 = mybir.dt.float8_e4m3fn_x4
ALU = mybir.AluOpType
ACT = mybir.ActivationFunctionType

P = 128
PACK = 4
GROUP = 4
STRIPE = 16
QUADRANT = 32
SLICE = 512
WINDOW = S + 32
SPANS = tuple(
    (t, lo, lo + width)
    for t in range(PACK)
    for width in [U // 2 if t in (0, PACK - 1) else U]
    for lo in range(0, U, width)
)
VECTOR_TILES = 2
PIECE = 256
SPANS_IN_FLIGHT = 3
ROCK_SHIFT = 0.4 + 1.5
LN_FLOOR = 2.0**-60
ROOT_FLOOR = 1e-30


def tile_picked_ygassm_imp_p_kernel(
    tc, x_words, x_scales, w1, w2, por, rho, unit, w3, offs, rk, fl, out
):
    nc = tc.nc
    with ExitStack() as ctx:
        keep = ctx.enter_context(tc.tile_pool(name="keep", bufs=1))
        work = ctx.enter_context(tc.tile_pool(name="work", bufs=2))
        ring = ctx.enter_context(tc.tile_pool(name="ring", bufs=SPANS_IN_FLIGHT))
        psum = ctx.enter_context(tc.psum_pool(name="psum", bufs=1))

        offs_t = keep.tile([P, S // STRIPE], U16, name="offs_t")
        rk_t = keep.tile([P, U // STRIPE], U16, name="rk_t")
        fl_t = keep.tile([P, U // STRIPE], U16, name="fl_t")
        xw = keep.tile([P, T], I32, name="xw", align_bytes=64)
        xs = keep.tile([P, T], U8, name="xs", align_bytes=64)
        nc.gpsimd.memset(xs[:].bitcast(I32), 0)
        nc.sync.dma_start(offs_t[:], offs)
        nc.sync.dma_start(xw[:], x_words[0].rearrange("p n t -> p (n t)").bitcast(I32))
        for q in range(P // QUADRANT):
            nc.sync.dma_start(
                xs[QUADRANT * q : QUADRANT * q + 4, :].bitcast(I32),
                x_scales[0, 4 * q : 4 * q + 4, :].bitcast(I32),
            )
        w_raw = []
        for name, w in (("w1_raw", w1), ("w2_raw", w2)):
            raw = keep.tile([P, PACK, H], F32, name=name)
            nc.sync.dma_start(raw[:], w.rearrange("(p j) c -> p j c", j=PACK))
            w_raw.append(raw)
        nc.sync.dma_start(rk_t[:], rk)
        nc.sync.dma_start(fl_t[:], fl)
        por_v = por.rearrange("(p t) r -> p t r", t=PACK)
        rho_v = rho.rearrange("(p t) r -> p t r", t=PACK)
        por_t = {}
        rho_t = {}
        unit_t = keep.tile([P, PACK], F32, name="unit_t")
        w3_raw = keep.tile([P, PACK, N], F32, name="w3_raw")
        for t in range(PACK):
            for name, view, tiles in (("por", por_v, por_t), ("rho", rho_v, rho_t)):
                tiles[t] = keep.tile([P, U], F32, name="%s%d" % (name, t))
                nc.sync.dma_start(tiles[t][:], view[:, t, :])
            if t == 0:
                nc.sync.dma_start(unit_t[:], unit.rearrange("(p t) o -> p (t o)", t=PACK))
                nc.sync.dma_start(w3_raw[:], w3.rearrange("(p j) n -> p j n", j=PACK))

        rock_win = [keep.tile([P, WINDOW], F32, name="rock_win%d" % t) for t in range(PACK)]
        fluid_win = [keep.tile([P, WINDOW], F32, name="fluid_win%d" % t) for t in range(PACK)]
        for win in rock_win + fluid_win:
            nc.gpsimd.memset(win[:, S:], 0.0)

        gw = keep.tile([P, S], U32, name="gw", align_bytes=64)
        gs = keep.tile([P, S], U8, name="gs", align_bytes=64)
        nc.vector.tensor_copy(gw[:], xw[:].bitcast(U32).indirect(offs_t[:]))
        nc.vector.tensor_copy(gs[:], xs[:].indirect(offs_t[:]))

        def bank(b):
            return psum.tile([P, S], F32, name="bank%d" % b)

        banks = [bank(b) for b in range(2 * PACK)]
        sig = keep.tile([P, 2, PACK, S], F32, name="sig")
        for side in range(2):
            wb = keep.tile([P, PACK, P, PACK], BF16, name="wb%d" % side, align_bytes=64)
            nc.vector.tensor_copy(
                wb[:].rearrange("p t m j -> p m j t"),
                w_raw[side][:].rearrange("p j (m t) -> p m j t", t=PACK),
            )
            wq = keep.tile([P, H], U32, name="wq%d" % side, align_bytes=64)
            ws = keep.tile([P, H], U8, name="ws%d" % side, align_bytes=64)
            for t in range(PACK):
                nc.vector.quantize_mx(
                    out=wq[:, t * P : (t + 1) * P].bitcast(FP8X4),
                    scales=ws[:, t * P : (t + 1) * P],
                    in_=wb[:, t].rearrange("p m j -> p (m j)"),
                )
                nc.tensor.matmul_mx(
                    out=banks[2 * t + side][:],
                    lhsT=wq[:, t * P : (t + 1) * P].bitcast(FP8X4),
                    lhsT_scale=ws[:, t * P : (t + 1) * P],
                    rhs=gw[:].bitcast(FP8X4),
                    rhs_scale=gs[:],
                    start=True,
                    stop=True,
                )
                nc.scalar.activation(sig[:, side, t, :], banks[2 * t + side][:], ACT.Sigmoid, scale=-1.0)

        fluid = keep.tile([P, PACK, S], F32, name="sp_fluid")

        def softplus(t):
            nc.scalar.activation(sig[:, :, t, :], sig[:, :, t, :], ACT.Ln, bias=LN_FLOOR)
            nc.vector.scalar_tensor_tensor(
                fluid[:, t, :], sig[:, 1, t, :], -1.0, banks[2 * t + 1][:], ALU.mult, ALU.max
            )
            nc.vector.scalar_tensor_tensor(
                rock_win[t][:, :S], sig[:, 0, t, :], -1.0, banks[2 * t][:], ALU.mult, ALU.max
            )
            if t < VECTOR_TILES:
                nc.gpsimd.tensor_scalar(rock_win[t][:, :S], rock_win[t][:, :S], 1.0, ROCK_SHIFT, ALU.mult, ALU.add)

        def invert_fluid(t):
            nc.scalar.activation(fluid[:, t, :], fluid[:, t, :], ACT.Abs_reciprocal_sqrt, scale=0.5, bias=0.1)
            nc.gpsimd.tensor_tensor(fluid_win[t][:, :S], fluid[:, t, :], fluid[:, t, :], ALU.mult)

        w3q = keep.tile([P, N], U32, name="w3q", align_bytes=64)
        w3s = keep.tile([P, N], U8, name="w3s", align_bytes=64)
        unit_fifth = keep.tile([P, PACK], F32, name="fifth")
        unit_squared = keep.tile([P, PACK], F32, name="squared")
        unit_shift = keep.tile([P, PACK], F32, name="shift")
        modulus = keep.tile([P, PACK, U], F32, name="modulus")
        span_tiles = {}
        woven = {}

        def prepare_unit_and_w3():
            unit_sign = keep.tile([P, PACK], F32, name="sign")
            nc.vector.tensor_scalar(unit_sign[:], unit_t[:], 0.0, 2.0, ALU.is_ge, ALU.mult)
            nc.vector.tensor_scalar(unit_sign[:], unit_sign[:], -1.0, None, ALU.add)
            nc.vector.tensor_scalar(unit_fifth[:], unit_t[:], 0.2, None, ALU.mult)
            nc.vector.tensor_tensor(unit_squared[:], unit_t[:], unit_t[:], ALU.mult)
            nc.vector.tensor_scalar(unit_shift[:], unit_squared[:], -1.5, None, ALU.mult)
            w3b = keep.tile([P, N, PACK], BF16, name="w3b", align_bytes=64)
            nc.vector.tensor_tensor(
                w3b[:],
                w3_raw[:].rearrange("p j n -> p n j"),
                unit_sign[:].unsqueeze(1).to_broadcast([P, N, PACK]),
                ALU.mult,
            )
            nc.vector.quantize_mx(
                out=w3q[:].bitcast(FP8X4), scales=w3s[:], in_=w3b[:].rearrange("p n j -> p (n j)")
            )

        def fetch(i):
            t, lo, hi = SPANS[i]
            a = ring.tile([P, hi - lo], F32, name="a")
            den = ring.tile([P, hi - lo], F32, name="x")
            for c in range(lo, hi, SLICE):
                picked = fluid_win[t][:].indirect(fl_t[:, c // STRIPE : (c + SLICE) // STRIPE])
                nc.scalar.activation(den[:, c - lo : c - lo + SLICE], picked, ACT.Copy)
            for c in range(lo, hi, SLICE):
                picked = rock_win[t][:].indirect(rk_t[:, c // STRIPE : (c + SLICE) // STRIPE])
                if t < VECTOR_TILES:
                    nc.vector.tensor_copy(a[:, c - lo : c - lo + SLICE], picked)
                else:
                    nc.scalar.activation(a[:, c - lo : c - lo + SLICE], picked, ACT.Copy, bias=ROCK_SHIFT)
            span_tiles[i] = (a, den)

        def denominator(i):
            t, lo, hi = SPANS[i]
            a, den = span_tiles[i]
            nc.vector.scalar_tensor_tensor(den[:], den[:], -0.3, por_t[t][:, lo:hi], ALU.add, ALU.mult)
            nc.vector.scalar_tensor_tensor(den[:], den[:], 0.06, a[:], ALU.add, ALU.mult)
            nc.vector.scalar_tensor_tensor(den[:], den[:], 0.36, a[:], ALU.add, ALU.mult)
            term = ring.tile([P, hi - lo], F32, name="y")
            nc.scalar.activation(term[:], den[:], ACT.Abs_reciprocal_sqrt, bias=ROOT_FLOOR)
            nc.scalar.activation(den[:], den[:], ACT.Sign)
            span_tiles[i] = (a, den, term)

        def quotient(i):
            t = SPANS[i][0]
            a, den_sign, term = span_tiles[i]
            nc.vector.scalar_tensor_tensor(term[:], a[:], 6.0, term[:], ALU.add, ALU.mult)
            nc.scalar.activation(term[:], term[:], ACT.Square, scale=unit_fifth[:, t : t + 1])

        def saturate(i):
            t, lo, hi = SPANS[i]
            a, den_sign, term = span_tiles[i]
            nc.vector.tensor_tensor(term[:], term[:], den_sign[:], ALU.mult)
            nc.vector.scalar_tensor_tensor(term[:], a[:], unit_squared[:, t : t + 1], term[:], ALU.mult, ALU.add)
            nc.vector.scalar_tensor_tensor(
                modulus[:, t, lo:hi], term[:], unit_shift[:, t : t + 1], rho_t[t][:, lo:hi], ALU.add, ALU.mult
            )

        def weave(h):
            imp = keep.tile([P, GROUP, PIECE // GROUP, PACK], F32, name="imp%d" % h)
            nc.scalar.activation(
                imp[:].rearrange("p d g t -> p g t d"),
                modulus[:, :, h * PIECE : (h + 1) * PIECE].rearrange("p t (g d) -> p g t d", d=GROUP),
                ACT.Sqrt,
            )
            woven[h] = imp

        def finish(h):
            members = woven[h][:].rearrange("p d g t -> p d (g t)")
            sums = work.tile([P, 2, PIECE], F32, name="pair")
            nc.vector.tensor_tensor(sums[:], members[:, 0:2, :], members[:, 2:4, :], ALU.add)
            nc.vector.tensor_tensor(sums[:, 0, :], sums[:, 0, :], sums[:, 1, :], ALU.add)
            hid = work.tile([P, GROUP, PIECE], BF16, name="hid", align_bytes=64)
            nc.vector.scalar_tensor_tensor(
                hid[:], sums[:, 0:1, :].to_broadcast([P, GROUP, PIECE]), -0.2, members, ALU.mult, ALU.add
            )
            hq = work.tile([P, PIECE], U32, name="hq", align_bytes=64)
            hs = work.tile([P, PIECE], U8, name="hs", align_bytes=64)
            nc.vector.quantize_mx(
                out=hq[:].bitcast(FP8X4), scales=hs[:], in_=hid[:].rearrange("p d c -> p (d c)")
            )
            acc = bank(h % 2)
            nc.tensor.matmul_mx(
                out=acc[:, :PIECE],
                lhsT=w3q[:].bitcast(FP8X4),
                lhsT_scale=w3s[:],
                rhs=hq[:].bitcast(FP8X4),
                rhs_scale=hs[:],
                start=True,
                stop=True,
            )
            res = work.tile([P, PIECE // GROUP, GROUP], F32, name="res")
            nc.scalar.copy(res[:], acc[:, :PIECE].rearrange("p (d g) -> p g d", d=GROUP))
            nc.sync.dma_start(out[:, h * PIECE : (h + 1) * PIECE], res[:].rearrange("p g d -> p (g d)"))

        prepare_unit_and_w3()
        for t in range(PACK):
            softplus(t)
        for t in range(PACK):
            invert_fluid(t)
        for step in range(len(SPANS) + 3):
            for stage, lag in ((fetch, 0), (saturate, 3), (quotient, 2), (denominator, 1)):
                if 0 <= step - lag < len(SPANS):
                    stage(step - lag)
        for h in range(U // PIECE):
            weave(h)
        for h in range(U // PIECE):
            finish(h)
